import numpy as np
import ml_dtypes


def mxq(x, axis, fmt="e4m3"):
    dtype, down = {"e4m3": (ml_dtypes.float8_e4m3fn, 7), "e5m2": (ml_dtypes.float8_e5m2, 14)}[fmt]
    v = np.moveaxis(np.asarray(x, np.float32).astype(ml_dtypes.bfloat16).astype(np.float64), axis, -1)
    blocks = v.reshape(v.shape[:-1] + (-1, 32))
    amax = np.abs(blocks).max(-1, keepdims=True)
    byte = np.maximum(np.where(amax > 0, np.frexp(amax)[1] - 1 + 127, 0) - down, 1)
    scale = np.exp2(byte - 127.0)
    codes = (blocks / scale).astype(np.float32).astype(dtype).astype(np.float64)
    return np.moveaxis((codes * scale).reshape(v.shape), -1, axis)


WIDE = False


def mx_kscale(k):
    if not WIDE:
        return np.ones(k)
    levels = np.array([10, -10, 5, -5, 0])
    if k % 512:
        return np.exp2(np.random.permutation(np.resize(levels, k // 32))).repeat(32)
    a = np.empty((k // 512, 16))
    for p in range(k // 512):
        a[p, :8] = np.random.permutation(np.resize(levels, 8))
        for g in range(8):
            far = levels[np.abs(levels - a[p, g]) >= 10]
            a[p, g + 8] = far[np.random.randint(len(far))]
    return np.exp2(a.ravel()).repeat(32)


def f64(x):
    return np.asarray(x).astype(np.float64)


def striped(idx):
    return np.tile(idx.reshape(-1, 16).T, (8, 1)).astype(np.uint16)


def unstriped(offs):
    return offs[:16].T.reshape(-1).astype(np.int64)


def pack_weight(w):
    k, n = w.shape
    w = f64(np.asarray(w, np.float32).astype(ml_dtypes.bfloat16)).reshape(k // 32, 32, n)
    amax = np.abs(w).max(1)
    byte = np.clip(np.where(amax > 0, np.frexp(amax)[1] - 1 + 127 - 7, 1), 1, 254)
    scaled = (w * np.exp2(127.0 - byte)[:, None, :]).reshape(k, n).astype(np.float32)
    words = np.ascontiguousarray(scaled.reshape(k // 512, 128, 4, n).transpose(0, 1, 3, 2)).astype(ml_dtypes.float8_e4m3fn).view(np.uint8)
    return words, np.ascontiguousarray(byte.astype(np.uint8).reshape(k // 512, 16, n))


def unpack_weight(words, scales):
    g, p, n, _ = words.shape
    vals = np.ascontiguousarray(words).view(ml_dtypes.float8_e4m3fn).astype(np.float64) * np.repeat(np.exp2(scales.astype(np.float64) - 127.0), 8, axis=1)[..., None]
    return vals.transpose(0, 1, 3, 2).reshape(g * 512, n)


def gelu(v):
    return 0.5 * v * (1.0 + np.tanh(np.sqrt(2.0 / np.pi) * (v + 0.044715 * v**3)))


K, T, S, N = 512, 2048, 512, 512


def setup_inputs():
    n = np.random.standard_normal
    s = mx_kscale(K)[:, None]
    w1, w2 = n((2, K, N)) / np.sqrt(2 * K) / s[None]
    p1, p2 = pack_weight(w1), pack_weight(w2)
    return {
        "xT": (n((K, S)) * s).astype(np.float32),
        "sT": (n((K, T)) * s).astype(np.float32),
        "w1_words": p1[0],
        "w1_scales": p1[1],
        "w2_words": p2[0],
        "w2_scales": p2[1],
        "b": (0.3 * n((N, 1))).astype(np.float32),
        "offs": striped(np.random.permutation(T)[:S]),
    }


def reference(xT, sT, w1_words, w1_scales, w2_words, w2_scales, b, offs):
    y = unpack_weight(w1_words, w1_scales).T @ mxq(f64(xT), 0, "e4m3") + unpack_weight(w2_words, w2_scales).T @ mxq(f64(sT)[:, unstriped(offs)], 0, "e4m3")
    return gelu(y + f64(b))

@@ -1,0 +1,137 @@
+from contextlib import ExitStack
+
+import concourse.mybir as mybir
+from concourse.masks import make_identity
+
+P = 128
+K = 512
+T = 2048
+S = 512
+N = 512
+PACK = 4
+HALF = 256
+M_TILES = N // P
+FLOPS = 2 * 2 * K * N * S
+
+F32 = mybir.dt.float32
+BF16 = mybir.dt.bfloat16
+I32 = mybir.dt.int32
+U32 = mybir.dt.uint32
+U16 = mybir.dt.uint16
+U8 = mybir.dt.uint8
+FP8X4 = mybir.dt.float8_e4m3fn_x4
+GELU = mybir.ActivationFunctionType.Gelu_apprx_tanh
+
+
+def tile_picked_recall_gelu_e_kernel(tc, xT, sT, w1_words, w1_scales, w2_words, w2_scales, b, offs, out):
+    nc = tc.nc
+    with ExitStack() as ctx:
+        held = ctx.enter_context(tc.tile_pool(name="held", bufs=1))
+        psum = ctx.enter_context(tc.psum_pool(name="psum", bufs=1))
+
+        offsets = held.tile([P, S // 16], U16, name="offsets")
+        planes = [held.tile([P, T], F32, name="plane%d" % t, align_bytes=64) for t in range(PACK)]
+        words1 = held.tile([P, N], I32, name="words1", align_bytes=64)
+        words2 = held.tile([P, N], I32, name="words2", align_bytes=64)
+        scales1 = held.tile([P, N], U8, name="scales1", align_bytes=64)
+        scales2 = held.tile([P, N], U8, name="scales2", align_bytes=64)
+        bias_rows = held.tile([P, P], F32, name="bias_rows")
+        bias = held.tile([P, M_TILES], F32, name="bias")
+        ident = held.tile([P, P], F32, name="ident")
+        dummy = held.tile([P, 2], F32, name="dummy")
+
+        s_rows = sT.rearrange("(p t) c -> t p c", t=PACK)
+        x_rows = xT.rearrange("(p j) n -> p j n", j=PACK)
+
+        nc.vector.memset(scales2[:].bitcast(I32), 0)
+        nc.vector.memset(scales1[:].bitcast(I32), 0)
+        nc.vector.memset(dummy[:], 0.0)
+        nc.vector.memset(bias_rows[:], 0.0)
+        make_identity(nc, ident[:])
+
+        def load_scale_rows(queue, scales, source):
+            for q in range(4):
+                queue.dma_start(
+                    scales[32 * q : 32 * q + 4, :].bitcast(I32),
+                    source[0, 4 * q : 4 * q + 4, :].bitcast(I32),
+                )
+
+        nc.sync.dma_start(planes[0][:], s_rows[0])
+        nc.sync.dma_start(offsets[:], offs)
+        nc.sync.dma_start(planes[1][:], s_rows[1])
+        nc.sync.dma_start(planes[2][:], s_rows[2])
+        nc.scalar.activation(dummy[:, 1:2], dummy[:, 0:1], GELU)
+        load_scale_rows(nc.gpsimd, scales2, w2_scales)
+        nc.gpsimd.dma_start(bias_rows[0:M_TILES, :], b.rearrange("(m p) o -> m (p o)", p=P))
+        load_scale_rows(nc.scalar, scales1, w1_scales)
+        nc.sync.dma_start(planes[3][:], s_rows[3])
+        nc.sync.dma_start(words2[:], w2_words[0].rearrange("p m r -> p (m r)").bitcast(I32))
+        nc.sync.dma_start(words1[:], w1_words[0].rearrange("p m r -> p (m r)").bitcast(I32))
+        x_raw = []
+        for h in range(2):
+            raw = held.tile([P, PACK, HALF], F32, name="x_raw%d" % h, align_bytes=64)
+            nc.sync.dma_start(raw[:], x_rows[:, :, h * HALF : (h + 1) * HALF])
+            x_raw.append(raw)
+
+        turned = psum.tile([P, P], F32, name="turned", tag="acc7")
+        nc.tensor.transpose(turned[:], bias_rows[:], ident[:])
+        nc.vector.tensor_copy(bias[:], turned[:, 0:M_TILES])
+
+        s_mix = held.tile([P, S, PACK], BF16, name="s_mix", align_bytes=64)
+        for t in range(PACK - 1):
+            nc.vector.tensor_copy(s_mix[:, :, t], planes[t][:].indirect(offsets[:]))
+        for h in range(2):
+            nc.vector.tensor_copy(
+                s_mix[:, h * HALF : (h + 1) * HALF, PACK - 1],
+                planes[PACK - 1][:].indirect(offsets[:, h * 16 : (h + 1) * 16]),
+            )
+
+        s_codes, s_scales, x_codes, x_scales = [], [], [], []
+        for h in range(2):
+            codes = held.tile([P, HALF], U32, name="s_codes%d" % h, align_bytes=64)
+            scales = held.tile([P, HALF], U8, name="s_scales%d" % h, align_bytes=64)
+            nc.vector.quantize_mx(
+                out=codes[:].bitcast(FP8X4),
+                scales=scales[:],
+                in_=s_mix[:, h * HALF : (h + 1) * HALF, :].rearrange("p n t -> p (n t)"),
+            )
+            s_codes.append(codes)
+            s_scales.append(scales)
+
+        accs = []
+        for h in range(2):
+            for m in range(M_TILES):
+                acc = psum.tile([P, HALF], F32, name="acc%d" % (h * M_TILES + m), tag="acc%d" % (h * M_TILES + m))
+                nc.tensor.matmul_mx(
+                    out=acc[:],
+                    lhsT=words2[:, m * P : (m + 1) * P].bitcast(FP8X4),
+                    lhsT_scale=scales2[:, m * P : (m + 1) * P],
+                    rhs=s_codes[h][:].bitcast(FP8X4),
+                    rhs_scale=s_scales[h][:],
+                    start=True,
+                    stop=False,
+                )
+                accs.append(acc)
+
+        for h in range(2):
+            mix = held.tile([P, HALF, PACK], BF16, name="x_mix%d" % h, align_bytes=64)
+            nc.vector.tensor_copy(mix[:], x_raw[h][:].rearrange("p j n -> p n j"))
+            codes = held.tile([P, HALF], U32, name="x_codes%d" % h, align_bytes=64)
+            scales = held.tile([P, HALF], U8, name="x_scales%d" % h, align_bytes=64)
+            nc.vector.quantize_mx(out=codes[:].bitcast(FP8X4), scales=scales[:], in_=mix[:].rearrange("p n t -> p (n t)"))
+            x_codes.append(codes)
+            x_scales.append(scales)
+            for m in range(M_TILES):
+                acc = accs[h * M_TILES + m]
+                nc.tensor.matmul_mx(
+                    out=acc[:],
+                    lhsT=words1[:, m * P : (m + 1) * P].bitcast(FP8X4),
+                    lhsT_scale=scales1[:, m * P : (m + 1) * P],
+                    rhs=codes[:].bitcast(FP8X4),
+                    rhs_scale=scales[:],
+                    start=False,
+                    stop=True,
+                )
+                result = held.tile([P, HALF], F32, name="result%d" % (h * M_TILES + m))
+                nc.scalar.activation(result[:], acc[:], GELU, bias=bias[:, m : m + 1])
+                nc.sync.dma_start(out[m * P : (m + 1) * P, h * HALF : (h + 1) * HALF], result[:])

@@ -56,6 +56,7 @@ def tile_picked_recall_gelu_e_kernel(tc, xT, sT, w1_words, w1_scales, w2_words, 
                     source[0, 4 * q : 4 * q + 4, :].bitcast(I32),
                 )
 
+        x_raw = held.tile([P, PACK, S], F32, name="x_raw", align_bytes=64)
         nc.sync.dma_start(planes[0][:], s_rows[0])
         nc.sync.dma_start(offsets[:], offs)
         nc.sync.dma_start(planes[1][:], s_rows[1])
@@ -66,12 +67,8 @@ def tile_picked_recall_gelu_e_kernel(tc, xT, sT, w1_words, w1_scales, w2_words, 
         load_scale_rows(nc.scalar, scales1, w1_scales)
         nc.sync.dma_start(planes[3][:], s_rows[3])
         nc.sync.dma_start(words2[:], w2_words[0].rearrange("p m r -> p (m r)").bitcast(I32))
+        nc.sync.dma_start(x_raw[:], x_rows)
         nc.sync.dma_start(words1[:], w1_words[0].rearrange("p m r -> p (m r)").bitcast(I32))
-        x_raw = []
-        for h in range(2):
-            raw = held.tile([P, PACK, HALF], F32, name="x_raw%d" % h, align_bytes=64)
-            nc.sync.dma_start(raw[:], x_rows[:, :, h * HALF : (h + 1) * HALF])
-            x_raw.append(raw)
 
         turned = psum.tile([P, P], F32, name="turned", tag="acc7")
         nc.tensor.transpose(turned[:], bias_rows[:], ident[:])
@@ -113,12 +110,14 @@ def tile_picked_recall_gelu_e_kernel(tc, xT, sT, w1_words, w1_scales, w2_words, 
                 )
                 accs.append(acc)
 
+        mixes = [held.tile([P, HALF, PACK], BF16, name="x_mix%d" % h, align_bytes=64) for h in range(2)]
+        nc.vector.tensor_copy(mixes[0][:, 0:P, :], x_raw[:, :, 0:P].rearrange("p j n -> p n j"))
+        nc.scalar.copy(mixes[0][:, P:HALF, :], x_raw[:, :, P:HALF].rearrange("p j n -> p n j"))
+        nc.vector.tensor_copy(mixes[1][:], x_raw[:, :, HALF:S].rearrange("p j n -> p n j"))
         for h in range(2):
-            mix = held.tile([P, HALF, PACK], BF16, name="x_mix%d" % h, align_bytes=64)
-            nc.vector.tensor_copy(mix[:], x_raw[h][:].rearrange("p j n -> p n j"))
             codes = held.tile([P, HALF], U32, name="x_codes%d" % h, align_bytes=64)
             scales = held.tile([P, HALF], U8, name="x_scales%d" % h, align_bytes=64)
-            nc.vector.quantize_mx(out=codes[:].bitcast(FP8X4), scales=scales[:], in_=mix[:].rearrange("p n t -> p (n t)"))
+            nc.vector.quantize_mx(out=codes[:].bitcast(FP8X4), scales=scales[:], in_=mixes[h][:].rearrange("p n t -> p (n t)"))
             x_codes.append(codes)
             x_scales.append(scales)
             for m in range(M_TILES):

@@ -43,11 +43,14 @@ def tile_picked_recall_gelu_e_kernel(tc, xT, sT, w1_words, w1_scales, w2_words, 
         s_rows = sT.rearrange("(p t) c -> t p c", t=PACK)
         x_rows = xT.rearrange("(p j) n -> p j n", j=PACK)
 
+        nc.gpsimd.memset(scales1[:].bitcast(I32), 0)
         nc.vector.memset(scales2[:].bitcast(I32), 0)
-        nc.vector.memset(scales1[:].bitcast(I32), 0)
         nc.vector.memset(dummy[:], 0.0)
         nc.vector.memset(bias_rows[:], 0.0)
         make_identity(nc, ident[:])
+
+        pieces = ((0, 256), (256, 128), (384, 128))
+        x_raw = [held.tile([P, PACK, n], F32, name="x_raw%d" % c, align_bytes=64) for c, n in pieces]
 
         def load_scale_rows(queue, scales, source):
             for q in range(4):
@@ -56,19 +59,32 @@ def tile_picked_recall_gelu_e_kernel(tc, xT, sT, w1_words, w1_scales, w2_words, 
                     source[0, 4 * q : 4 * q + 4, :].bitcast(I32),
                 )
 
-        x_raw = held.tile([P, PACK, S], F32, name="x_raw", align_bytes=64)
+        def load_x(i):
+            c, n = pieces[i]
+            nc.sync.dma_start(x_raw[i][:], x_rows[:, :, c : c + n])
+
         nc.sync.dma_start(planes[0][:], s_rows[0])
         nc.sync.dma_start(offsets[:], offs)
         nc.sync.dma_start(planes[1][:], s_rows[1])
+        load_scale_rows(nc.scalar, scales1, w1_scales)
         nc.sync.dma_start(planes[2][:], s_rows[2])
-        nc.scalar.activation(dummy[:, 1:2], dummy[:, 0:1], GELU)
         load_scale_rows(nc.gpsimd, scales2, w2_scales)
         nc.gpsimd.dma_start(bias_rows[0:M_TILES, :], b.rearrange("(m p) o -> m (p o)", p=P))
-        load_scale_rows(nc.scalar, scales1, w1_scales)
+        nc.scalar.activation(dummy[:, 1:2], dummy[:, 0:1], GELU)
+        load_x(0)
         nc.sync.dma_start(planes[3][:], s_rows[3])
-        nc.sync.dma_start(words2[:], w2_words[0].rearrange("p m r -> p (m r)").bitcast(I32))
-        nc.sync.dma_start(x_raw[:], x_rows)
         nc.sync.dma_start(words1[:], w1_words[0].rearrange("p m r -> p (m r)").bitcast(I32))
+        nc.sync.dma_start(words2[:], w2_words[0].rearrange("p m r -> p (m r)").bitcast(I32))
+        load_x(1)
+        load_x(2)
+
+        def quantise(mix, n, name):
+            codes = held.tile([P, n], U32, name=name + "_codes", align_bytes=64)
+            scales = held.tile([P, n], U8, name=name + "_scales", align_bytes=64)
+            nc.vector.quantize_mx(
+                out=codes[:].bitcast(FP8X4), scales=scales[:], in_=mix.rearrange("p n t -> p (n t)")
+            )
+            return codes, scales
 
         turned = psum.tile([P, P], F32, name="turned", tag="acc7")
         nc.tensor.transpose(turned[:], bias_rows[:], ident[:])
@@ -77,60 +93,54 @@ def tile_picked_recall_gelu_e_kernel(tc, xT, sT, w1_words, w1_scales, w2_words, 
         s_mix = held.tile([P, S, PACK], BF16, name="s_mix", align_bytes=64)
         for t in range(PACK - 1):
             nc.vector.tensor_copy(s_mix[:, :, t], planes[t][:].indirect(offsets[:]))
+        mix0 = held.tile([P, 256, PACK], BF16, name="x_mix0", align_bytes=64)
+        nc.scalar.copy(mix0[:], x_raw[0][:].rearrange("p j n -> p n j"))
+        x0_quant = quantise(mix0[:], 256, "x0")
         for h in range(2):
             nc.vector.tensor_copy(
                 s_mix[:, h * HALF : (h + 1) * HALF, PACK - 1],
                 planes[PACK - 1][:].indirect(offsets[:, h * 16 : (h + 1) * 16]),
             )
+        s_quant = [quantise(s_mix[:, h * HALF : (h + 1) * HALF, :], HALF, "s%d" % h) for h in range(2)]
 
-        s_codes, s_scales, x_codes, x_scales = [], [], [], []
-        for h in range(2):
-            codes = held.tile([P, HALF], U32, name="s_codes%d" % h, align_bytes=64)
-            scales = held.tile([P, HALF], U8, name="s_scales%d" % h, align_bytes=64)
-            nc.vector.quantize_mx(
-                out=codes[:].bitcast(FP8X4),
-                scales=scales[:],
-                in_=s_mix[:, h * HALF : (h + 1) * HALF, :].rearrange("p n t -> p (n t)"),
-            )
-            s_codes.append(codes)
-            s_scales.append(scales)
+        out_rows = out.rearrange("(m p) n -> p m n", p=P)
 
-        accs = []
-        for h in range(2):
+        def products(accs, words, scales, moving, lo, n, opens):
+            codes, plane = moving
             for m in range(M_TILES):
-                acc = psum.tile([P, HALF], F32, name="acc%d" % (h * M_TILES + m), tag="acc%d" % (h * M_TILES + m))
                 nc.tensor.matmul_mx(
-                    out=acc[:],
-                    lhsT=words2[:, m * P : (m + 1) * P].bitcast(FP8X4),
-                    lhsT_scale=scales2[:, m * P : (m + 1) * P],
-                    rhs=s_codes[h][:].bitcast(FP8X4),
-                    rhs_scale=s_scales[h][:],
-                    start=True,
-                    stop=False,
+                    out=accs[m][:],
+                    lhsT=words[:, m * P : (m + 1) * P].bitcast(FP8X4),
+                    lhsT_scale=scales[:, m * P : (m + 1) * P],
+                    rhs=codes[:, lo : lo + n].bitcast(FP8X4),
+                    rhs_scale=plane[:, lo : lo + n],
+                    start=opens,
+                    stop=not opens,
                 )
-                accs.append(acc)
 
-        mixes = [held.tile([P, HALF, PACK], BF16, name="x_mix%d" % h, align_bytes=64) for h in range(2)]
-        nc.vector.tensor_copy(mixes[0][:, 0:P, :], x_raw[:, :, 0:P].rearrange("p j n -> p n j"))
-        nc.scalar.copy(mixes[0][:, P:HALF, :], x_raw[:, :, P:HALF].rearrange("p j n -> p n j"))
-        nc.vector.tensor_copy(mixes[1][:], x_raw[:, :, HALF:S].rearrange("p j n -> p n j"))
-        for h in range(2):
-            codes = held.tile([P, HALF], U32, name="x_codes%d" % h, align_bytes=64)
-            scales = held.tile([P, HALF], U8, name="x_scales%d" % h, align_bytes=64)
-            nc.vector.quantize_mx(out=codes[:].bitcast(FP8X4), scales=scales[:], in_=mixes[h][:].rearrange("p n t -> p (n t)"))
-            x_codes.append(codes)
-            x_scales.append(scales)
-            for m in range(M_TILES):
-                acc = accs[h * M_TILES + m]
-                nc.tensor.matmul_mx(
-                    out=acc[:],
-                    lhsT=words1[:, m * P : (m + 1) * P].bitcast(FP8X4),
-                    lhsT_scale=scales1[:, m * P : (m + 1) * P],
-                    rhs=codes[:].bitcast(FP8X4),
-                    rhs_scale=scales[:],
-                    start=False,
-                    stop=True,
-                )
-                result = held.tile([P, HALF], F32, name="result%d" % (h * M_TILES + m))
-                nc.scalar.activation(result[:], acc[:], GELU, bias=bias[:, m : m + 1])
-                nc.sync.dma_start(out[m * P : (m + 1) * P, h * HALF : (h + 1) * HALF], result[:])
+        def banks(i):
+            n = pieces[i][1]
+            return [
+                psum.tile([P, n], F32, name="acc%d_%d" % (i, m), tag="acc%d" % ((i % 2) * M_TILES + m))
+                for m in range(M_TILES)
+            ]
+
+        def leave(i, accs):
+            c, n = pieces[i]
+            for m0 in range(0, M_TILES, 2):
+                result = held.tile([P, 2, n], F32, name="result%d_%d" % (i, m0))
+                for m in (m0, m0 + 1):
+                    nc.scalar.activation(result[:, m - m0, :], accs[m][:], GELU, bias=bias[:, m : m + 1])
+                nc.sync.dma_start(out_rows[:, m0 : m0 + 2, c : c + n], result[:])
+
+        accs = banks(0)
+        products(accs, words1, scales1, x0_quant, 0, 256, True)
+        products(accs, words2, scales2, s_quant[0], 0, 256, False)
+        leave(0, accs)
+        for i in (1, 2):
+            accs = banks(i)
+            products(accs, words2, scales2, s_quant[1], pieces[i][0] - HALF, P, True)
+            mix = held.tile([P, P, PACK], BF16, name="x_mix%d" % i, align_bytes=64)
+            nc.vector.tensor_copy(mix[:], x_raw[i][:].rearrange("p j n -> p n j"))
+            products(accs, words1, scales1, quantise(mix[:], P, "x%d" % i), 0, P, False)
+            leave(i, accs)

from contextlib import ExitStack

import concourse.mybir as mybir
from concourse.masks import make_identity

P = 128
K = 512
T = 2048
S = 512
N = 512
PACK = 4
HALF = 256
M_TILES = N // P
FLOPS = 2 * 2 * K * N * S

F32 = mybir.dt.float32
BF16 = mybir.dt.bfloat16
I32 = mybir.dt.int32
U32 = mybir.dt.uint32
U16 = mybir.dt.uint16
U8 = mybir.dt.uint8
FP8X4 = mybir.dt.float8_e4m3fn_x4
GELU = mybir.ActivationFunctionType.Gelu_apprx_tanh


def tile_picked_recall_gelu_e_kernel(tc, xT, sT, w1_words, w1_scales, w2_words, w2_scales, b, offs, out):
    nc = tc.nc
    with ExitStack() as ctx:
        held = ctx.enter_context(tc.tile_pool(name="held", bufs=1))
        psum = ctx.enter_context(tc.psum_pool(name="psum", bufs=1))

        offsets = held.tile([P, S // 16], U16, name="offsets")
        planes = [held.tile([P, T], F32, name="plane%d" % t, align_bytes=64) for t in range(PACK)]
        words1 = held.tile([P, N], I32, name="words1", align_bytes=64)
        words2 = held.tile([P, N], I32, name="words2", align_bytes=64)
        scales1 = held.tile([P, N], U8, name="scales1", align_bytes=64)
        scales2 = held.tile([P, N], U8, name="scales2", align_bytes=64)
        bias_rows = held.tile([P, P], F32, name="bias_rows")
        bias = held.tile([P, M_TILES], F32, name="bias")
        ident = held.tile([P, P], F32, name="ident")
        dummy = held.tile([P, 2], F32, name="dummy")

        s_rows = sT.rearrange("(p t) c -> t p c", t=PACK)
        x_rows = xT.rearrange("(p j) n -> p j n", j=PACK)

        nc.gpsimd.memset(scales1[:].bitcast(I32), 0)
        nc.vector.memset(scales2[:].bitcast(I32), 0)
        nc.vector.memset(dummy[:], 0.0)
        nc.vector.memset(bias_rows[:], 0.0)
        make_identity(nc, ident[:])

        pieces = ((0, 256), (256, 128), (384, 128))
        x_raw = [held.tile([P, PACK, n], F32, name="x_raw%d" % c, align_bytes=64) for c, n in pieces]

        def load_scale_rows(queue, scales, source):
            for q in range(4):
                queue.dma_start(
                    scales[32 * q : 32 * q + 4, :].bitcast(I32),
                    source[0, 4 * q : 4 * q + 4, :].bitcast(I32),
                )

        def load_x(i):
            c, n = pieces[i]
            nc.sync.dma_start(x_raw[i][:], x_rows[:, :, c : c + n])

        nc.sync.dma_start(planes[0][:], s_rows[0])
        nc.sync.dma_start(offsets[:], offs)
        nc.sync.dma_start(planes[1][:], s_rows[1])
        load_scale_rows(nc.scalar, scales1, w1_scales)
        nc.sync.dma_start(planes[2][:], s_rows[2])
        load_scale_rows(nc.gpsimd, scales2, w2_scales)
        nc.gpsimd.dma_start(bias_rows[0:M_TILES, :], b.rearrange("(m p) o -> m (p o)", p=P))
        nc.scalar.activation(dummy[:, 1:2], dummy[:, 0:1], GELU)
        load_x(0)
        nc.sync.dma_start(planes[3][:], s_rows[3])
        nc.sync.dma_start(words1[:], w1_words[0].rearrange("p m r -> p (m r)").bitcast(I32))
        nc.sync.dma_start(words2[:], w2_words[0].rearrange("p m r -> p (m r)").bitcast(I32))
        load_x(1)
        load_x(2)

        def quantise(mix, n, name):
            codes = held.tile([P, n], U32, name=name + "_codes", align_bytes=64)
            scales = held.tile([P, n], U8, name=name + "_scales", align_bytes=64)
            nc.vector.quantize_mx(
                out=codes[:].bitcast(FP8X4), scales=scales[:], in_=mix.rearrange("p n t -> p (n t)")
            )
            return codes, scales

        turned = psum.tile([P, P], F32, name="turned", tag="acc7")
        nc.tensor.transpose(turned[:], bias_rows[:], ident[:])
        nc.vector.tensor_copy(bias[:], turned[:, 0:M_TILES])

        s_mix = held.tile([P, S, PACK], BF16, name="s_mix", align_bytes=64)
        for t in range(PACK - 1):
            nc.vector.tensor_copy(s_mix[:, :, t], planes[t][:].indirect(offsets[:]))
        mix0 = held.tile([P, 256, PACK], BF16, name="x_mix0", align_bytes=64)
        nc.scalar.copy(mix0[:], x_raw[0][:].rearrange("p j n -> p n j"))
        x0_quant = quantise(mix0[:], 256, "x0")
        for h in range(2):
            nc.vector.tensor_copy(
                s_mix[:, h * HALF : (h + 1) * HALF, PACK - 1],
                planes[PACK - 1][:].indirect(offsets[:, h * 16 : (h + 1) * 16]),
            )
        s_quant = [quantise(s_mix[:, h * HALF : (h + 1) * HALF, :], HALF, "s%d" % h) for h in range(2)]

        out_rows = out.rearrange("(m p) n -> p m n", p=P)

        def products(accs, words, scales, moving, lo, n, opens):
            codes, plane = moving
            for m in range(M_TILES):
                nc.tensor.matmul_mx(
                    out=accs[m][:],
                    lhsT=words[:, m * P : (m + 1) * P].bitcast(FP8X4),
                    lhsT_scale=scales[:, m * P : (m + 1) * P],
                    rhs=codes[:, lo : lo + n].bitcast(FP8X4),
                    rhs_scale=plane[:, lo : lo + n],
                    start=opens,
                    stop=not opens,
                )

        def banks(i):
            n = pieces[i][1]
            return [
                psum.tile([P, n], F32, name="acc%d_%d" % (i, m), tag="acc%d" % ((i % 2) * M_TILES + m))
                for m in range(M_TILES)
            ]

        def leave(i, accs):
            c, n = pieces[i]
            for m0 in range(0, M_TILES, 2):
                result = held.tile([P, 2, n], F32, name="result%d_%d" % (i, m0))
                for m in (m0, m0 + 1):
                    nc.scalar.activation(result[:, m - m0, :], accs[m][:], GELU, bias=bias[:, m : m + 1])
                nc.sync.dma_start(out_rows[:, m0 : m0 + 2, c : c + n], result[:])

        accs = banks(0)
        products(accs, words1, scales1, x0_quant, 0, 256, True)
        products(accs, words2, scales2, s_quant[0], 0, 256, False)
        leave(0, accs)
        for i in (1, 2):
            accs = banks(i)
            products(accs, words2, scales2, s_quant[1], pieces[i][0] - HALF, P, True)
            mix = held.tile([P, P, PACK], BF16, name="x_mix%d" % i, align_bytes=64)
            nc.vector.tensor_copy(mix[:], x_raw[i][:].rearrange("p j n -> p n j"))
            products(accs, words1, scales1, quantise(mix[:], P, "x%d" % i), 0, P, False)
            leave(i, accs)
